import numpy as np
import ml_dtypes


def mxq(x, axis, fmt="e4m3"):
    dtype, down = {"e4m3": (ml_dtypes.float8_e4m3fn, 7), "e5m2": (ml_dtypes.float8_e5m2, 14)}[fmt]
    v = np.moveaxis(np.asarray(x, np.float32).astype(ml_dtypes.bfloat16).astype(np.float64), axis, -1)
    blocks = v.reshape(v.shape[:-1] + (-1, 32))
    amax = np.abs(blocks).max(-1, keepdims=True)
    byte = np.maximum(np.where(amax > 0, np.frexp(amax)[1] - 1 + 127, 0) - down, 1)
    scale = np.exp2(byte - 127.0)
    codes = (blocks / scale).astype(np.float32).astype(dtype).astype(np.float64)
    return np.moveaxis((codes * scale).reshape(v.shape), -1, axis)


WIDE = False


def mx_kscale(k):
    if not WIDE:
        return np.ones(k)
    levels = np.array([10, -10, 5, -5, 0])
    if k % 512:
        return np.exp2(np.random.permutation(np.resize(levels, k // 32))).repeat(32)
    a = np.empty((k // 512, 16))
    for p in range(k // 512):
        a[p, :8] = np.random.permutation(np.resize(levels, 8))
        for g in range(8):
            far = levels[np.abs(levels - a[p, g]) >= 10]
            a[p, g + 8] = far[np.random.randint(len(far))]
    return np.exp2(a.ravel()).repeat(32)


def f64(x):
    return np.asarray(x).astype(np.float64)


def striped(idx):
    return np.tile(idx.reshape(-1, 16).T, (8, 1)).astype(np.uint16)


def unstriped(offs):
    return offs[:16].T.reshape(-1).astype(np.int64)


def gelu(v):
    return 0.5 * v * (1.0 + np.tanh(np.sqrt(2.0 / np.pi) * (v + 0.044715 * v**3)))


K, T, E, C, N = 2048, 768, 6, 256, 256


def by_expert(wq, xq):
    return np.concatenate([wq[e].T @ xq[:, e * C:(e + 1) * C] for e in range(E)], axis=1)


def setup_inputs():
    n = np.random.standard_normal
    s = mx_kscale(K)[:, None]
    first = np.random.permutation(np.repeat(np.arange(E), T // E))
    second = (first + 1 + np.random.permutation(np.repeat(np.arange(E - 1), -(-T // (E - 1)))[:T])) % E
    while np.bincount(second, minlength=E).max() != T // E:
        load = np.bincount(second, minlength=E); hi, lo = int(load.argmax()), int(load.argmin())
        t = np.flatnonzero((second == hi) & (first != lo))[0]; second[t] = lo
    slot_token = np.empty(E * C, np.int64); pos = np.empty((2, T), np.int64); fill = np.zeros(E, np.int64)
    place = np.stack([np.random.permutation(C) for _ in range(E)])
    for r, deal in enumerate((first, second)):
        for t in np.random.permutation(T):
            e = deal[t]; j = e * C + place[e, fill[e]]; fill[e] += 1; slot_token[j] = t; pos[r, t] = j
    g = np.random.uniform(0.2, 0.8, T)
    w_slot = np.empty(E * C); w_slot[pos[0]] = g; w_slot[pos[1]] = 1.0 - g
    return {
        "xT": (n((K, T)) * s).astype(np.float32),
        "w": (n((E, K, N)) / np.sqrt(K) / s[None]).astype(np.float32),
        "b": (0.3 * n((N, E))).astype(np.float32),
        "gate": np.tile(w_slot, (K, 1)).astype(np.float32),
        "offs": striped(slot_token),
        "pos1": striped(pos[0]),
        "pos2": striped(pos[1]),
    }


def reference(xT, w, b, gate, offs, pos1, pos2):
    idx = unstriped(offs)
    xq = mxq(f64(gate) * f64(xT)[:, idx], 0, "e4m3")
    y = by_expert(mxq(f64(w), 1, "e4m3"), xq)
    y = gelu(y + np.repeat(f64(b), C, axis=1))
    return y[:, unstriped(pos1)] + y[:, unstriped(pos2)]

@@ -1,0 +1,230 @@
+from contextlib import ExitStack
+
+import concourse.mybir as mybir
+
+K, T, E, C, N = 2048, 768, 6, 256, 256
+S = E * C
+
+FLOPS = 2 * K * N * S
+BYTES = 4 * (K * T + E * K * N + N * E + S + N * T) + 2 * (S + 2 * T)
+
+F32 = mybir.dt.float32
+BF16 = mybir.dt.bfloat16
+U32 = mybir.dt.uint32
+U16 = mybir.dt.uint16
+U8 = mybir.dt.uint8
+FP8X4 = mybir.dt.float8_e4m3fn_x4
+MULT = mybir.AluOpType.mult
+ADD = mybir.AluOpType.add
+GELU = mybir.ActivationFunctionType.Gelu_apprx_tanh
+
+P = 128
+PACK = 4
+K_PASS = P * PACK
+PASSES = K // K_PASS
+HALVES = N // P
+STRIPE = 16
+GROUPS = 2
+E_GROUP = E // GROUPS
+S_GROUP = E_GROUP * C
+WINDOW = T + STRIPE
+RUN = 4
+
+
+def tile_moe_pre_lin_gelu_kernel(tc, xT, w, b, gate, offs, pos1, pos2, out):
+    nc = tc.nc
+    with ExitStack() as ctx:
+        held = ctx.enter_context(tc.tile_pool(name="held", bufs=1))
+        ring = ctx.enter_context(tc.tile_pool(name="ring", bufs=3))
+        psum = ctx.enter_context(tc.psum_pool(name="psum", bufs=8))
+
+        offs_sb = held.tile([P, S // STRIPE], U16, name="offs_sb")
+        pos_sb = [held.tile([P, T // STRIPE], U16, name="pos_sb%d" % r) for r in range(2)]
+        gate_sb = held.tile([P, S], F32, name="gate_sb")
+        bias_sb = [held.tile([P, E], F32, name="bias_sb%d" % h) for h in range(HALVES)]
+        tokens = [[held.tile([P, WINDOW], F32, name="tokens%d_%d" % (g, j)) for j in range(PACK)] for g in range(PASSES)]
+        y = [held.tile([P, S], F32, name="y%d" % h) for h in range(HALVES)]
+
+        w_late = held.tile([P, HALVES, PASSES, E_GROUP, P * PACK], BF16, name="w_late", align_bytes=64)
+        w_raw = {}
+        w_bf = {}
+        w_mx = {}
+        planes = {}
+        x_bf = {}
+        x_mx = {}
+        acc = {}
+
+        def load_tokens(g, j):
+            rows = xT[g * K_PASS : (g + 1) * K_PASS, :].rearrange("(p j) t -> p j t", j=PACK)
+            nc.sync.dma_start(tokens[g][j][:, 0:T], rows[:, j, :])
+
+        def load_gate(s0, s1):
+            nc.sync.dma_start(gate_sb[:, s0:s1], gate[0:P, s0:s1])
+
+        def load_w(grp, g, i):
+            raw = ring.tile([P, PACK, N], F32, name="w_raw", bufs=9)
+            rows = w[grp * E_GROUP + i, g * K_PASS : (g + 1) * K_PASS, :]
+            nc.sync.dma_start(raw[:], rows.rearrange("(p j) n -> p j n", j=PACK))
+            w_raw[grp, g, i] = raw
+
+        def round_w(grp, g):
+            if grp == 0:
+                grouped = ring.tile([P, HALVES, E_GROUP, P * PACK], BF16, name="w_bf", bufs=3, align_bytes=64)
+                w_bf[grp, g] = grouped[:].rearrange("p h i c -> p (h i c)")
+            else:
+                grouped = w_late[:, :, g, :, :]
+                w_bf[grp, g] = w_late[:, 0, g, :, :].rearrange("p i c -> p (i c)")
+            for i in range(E_GROUP):
+                nc.scalar.copy(
+                    grouped[:, :, i, :].rearrange("p h (c r j) -> p h c j r", r=RUN, j=PACK),
+                    w_raw[grp, g, i][:].rearrange("p j (h c r) -> p h c j r", h=HALVES, r=RUN),
+                )
+
+        def quantise(values, codes, scales, c0, c1):
+            nc.vector.quantize_mx(
+                out=codes[:, c0:c1].bitcast(FP8X4), scales=scales[:, c0:c1], in_=values[:, PACK * c0 : PACK * c1]
+            )
+
+        def quantise_w(grp, g, cuts):
+            codes = ring.tile([P, E_GROUP * N], U32, name="w_codes", align_bytes=64)
+            scales = ring.tile([P, E_GROUP * N], U8, name="w_scales", align_bytes=64)
+            for h in range(HALVES):
+                cols = slice(h * E_GROUP * P, (h + 1) * E_GROUP * P)
+                w_mx[grp, g, h] = (codes[:, cols], scales[:, cols])
+            for c0, c1 in cuts:
+                quantise(w_bf[grp, g], codes, scales, c0, c1)
+
+        def gather_x(grp, g, s0, s1):
+            a0, a1 = grp * S_GROUP + s0, grp * S_GROUP + s1
+            return [(planes[grp, g, s0, s1][:, j, :], tokens[g][j], a0, a1) for j in range(PACK)]
+
+        def run_gathers(jobs):
+            for dst, window, a0, a1 in jobs:
+                picked = window[:].indirect(offs_sb[:, a0 // STRIPE : a1 // STRIPE])
+                nc.vector.tensor_tensor(dst, picked, gate_sb[:, a0:a1], MULT)
+
+        def round_x(grp, g, s0, s1):
+            if (grp, g) not in x_bf:
+                x_bf[grp, g] = ring.tile([P, S_GROUP * PACK], BF16, name="x_bf", bufs=2, align_bytes=64)
+            nc.scalar.copy(
+                x_bf[grp, g][:, PACK * s0 : PACK * s1].rearrange("p (c r j) -> p c j r", r=RUN, j=PACK),
+                planes[grp, g, s0, s1].rearrange("p j (c r) -> p c j r", r=RUN),
+            )
+
+        def quantise_x(grp, g, s0, s1):
+            if (grp, g) not in x_mx:
+                codes = ring.tile([P, S_GROUP], U32, name="x_codes", bufs=5, align_bytes=64)
+                scales = ring.tile([P, S_GROUP], U8, name="x_scales", bufs=5, align_bytes=64)
+                x_mx[grp, g] = (codes, scales)
+            quantise(x_bf[grp, g][:], x_mx[grp, g][0], x_mx[grp, g][1], s0, s1)
+
+        def multiply(grp, g, i, h):
+            e = grp * E_GROUP + i
+            if g == 0:
+                acc[e, h] = psum.tile([P, C], F32, name="acc")
+            w_cols = slice(i * P, (i + 1) * P)
+            x_cols = slice(i * C, (i + 1) * C)
+            nc.tensor.matmul_mx(
+                out=acc[e, h][:],
+                lhsT=w_mx[grp, g, h][0][:, w_cols].bitcast(FP8X4),
+                lhsT_scale=w_mx[grp, g, h][1][:, w_cols],
+                rhs=x_mx[grp, g][0][:, x_cols].bitcast(FP8X4),
+                rhs_scale=x_mx[grp, g][1][:, x_cols],
+                start=(g == 0),
+                stop=(g == PASSES - 1),
+            )
+            if g == PASSES - 1:
+                nc.scalar.activation(y[h][:, e * C : (e + 1) * C], acc[e, h][:], GELU, bias=bias_sb[h][:, e : e + 1])
+
+        two, three = 2 * C, 3 * C
+        half = E_GROUP * P
+        cuts_whole = [(0, two), (two, three)]
+        cuts_x = [(0, C), (C, three)]
+        cuts_first = [(0, C), (C, half)]
+        last = (GROUPS - 1, PASSES - 1)
+        steps = [(grp, g) for grp in range(GROUPS) for g in range(PASSES)]
+
+        load_tokens(0, 0)
+        nc.sync.dma_start(offs_sb[:], offs)
+        load_gate(0, C)
+        load_gate(C, S_GROUP)
+        blocks = [(g, j) for g in range(PASSES) for j in range(PACK)]
+        matrices = [(0, g, i) for g in range(PASSES) for i in range(E_GROUP)]
+        lead = len(blocks) - len(matrices)
+        for m, block in enumerate(blocks):
+            if m > 0:
+                load_tokens(*block)
+            if m >= lead:
+                load_w(*matrices[m - lead])
+        load_gate(S_GROUP, S)
+        for h in range(HALVES):
+            nc.sync.dma_start(bias_sb[h][:], b[h * P : (h + 1) * P, :])
+        nc.sync.dma_start(pos_sb[0][:], pos1)
+        nc.sync.dma_start(pos_sb[1][:], pos2)
+        for g in range(PASSES):
+            for i in range(E_GROUP):
+                load_w(1, g, i)
+
+        def finish(grp, g):
+            for s0, s1 in cuts_whole if (grp, g) == last else cuts_x:
+                quantise_x(grp, g, s0, s1)
+            quantise_w(grp, g, cuts_whole if grp == 0 else cuts_first)
+            for i in range(E_GROUP):
+                for h in range(HALVES if grp == 0 else 1):
+                    multiply(grp, g, i, h)
+
+        for n, (grp, g) in enumerate(steps):
+            gathered = ring.tile([P, PACK, S_GROUP], F32, name="planes")
+            for s0, s1 in [(0, C), (C, three), (0, two), (0, three)]:
+                planes[grp, g, s0, s1] = gathered[:, :, s0:s1]
+            if n == 0:
+                round_w(grp, g)
+                small = gather_x(grp, g, 0, C)
+                rest = gather_x(grp, g, C, three)
+                whole = gather_x(grp, g, 0, three)
+                run_gathers([small[0], rest[0]] + whole[1:])
+            elif (grp, g) == last:
+                run_gathers(gather_x(grp, g, 0, two))
+                round_x(grp, g, 0, two)
+            else:
+                run_gathers(gather_x(grp, g, 0, three))
+            if (grp, g) != last:
+                for s0, s1 in cuts_x:
+                    round_x(grp, g, s0, s1)
+                round_w(*steps[n + 1])
+            if n > 0:
+                finish(*steps[n - 1])
+        grp, g = last
+        tail_planes = held.tile([P, PACK, C], F32, name="tail", align_bytes=64)
+        planes[grp, g, two, three] = tail_planes[:]
+        run_gathers(gather_x(grp, g, two, three))
+        round_x(grp, g, two, three)
+        finish(grp, g)
+        late_codes = held.tile([P, PASSES * half], U32, name="tail", align_bytes=64)
+        late_scales = held.tile([P, PASSES * half], U8, name="late_scales", align_bytes=64)
+        late_values = w_late[:, 1, :, :, :].rearrange("p g i c -> p (g i c)")
+        for c0 in range(0, PASSES * half, C):
+            quantise(late_values, late_codes, late_scales, c0, c0 + C)
+        for g in range(PASSES):
+            cols = slice(g * half, (g + 1) * half)
+            w_mx[grp, g, 1] = (late_codes[:, cols], late_scales[:, cols])
+            for i in range(E_GROUP):
+                multiply(grp, g, i, 1)
+
+        def fetch(h, t0, t1):
+            pair = ring.tile([P, 2, t1 - t0], F32, name="planes")
+            for r in range(2):
+                nc.vector.tensor_copy(pair[:, r, :], y[h][:].indirect(pos_sb[r][:, t0 // STRIPE : t1 // STRIPE]))
+            return pair
+
+        def add_and_store(pair, h, t0, t1):
+            nc.vector.tensor_tensor(pair[:, 0, :], pair[:, 0, :], pair[:, 1, :], ADD)
+            nc.sync.dma_start(out[h * P : (h + 1) * P, t0:t1], pair[:, 0, :])
+
+        pieces = [(0, 0, T), (1, 0, two), (1, two, T)]
+        pairs = []
+        for n, piece in enumerate(pieces):
+            pairs.append(fetch(*piece))
+            if n > 0:
+                add_and_store(pairs[n - 1], *pieces[n - 1])
+        add_and_store(pairs[-1], *pieces[-1])

@@ -104,10 +104,8 @@ def tile_moe_pre_lin_gelu_kernel(tc, xT, w, b, gate, offs, pos1, pos2, out):
                 nc.vector.tensor_tensor(dst, picked, gate_sb[:, a0:a1], MULT)
 
         def round_x(grp, g, s0, s1):
-            if (grp, g) not in x_bf:
-                x_bf[grp, g] = ring.tile([P, S_GROUP * PACK], BF16, name="x_bf", bufs=2, align_bytes=64)
             nc.scalar.copy(
-                x_bf[grp, g][:, PACK * s0 : PACK * s1].rearrange("p (c r j) -> p c j r", r=RUN, j=PACK),
+                x_bf[grp, g, s0, s1].rearrange("p (c r j) -> p c j r", r=RUN, j=PACK),
                 planes[grp, g, s0, s1].rearrange("p j (c r) -> p c j r", r=RUN),
             )
 
@@ -116,7 +114,10 @@ def tile_moe_pre_lin_gelu_kernel(tc, xT, w, b, gate, offs, pos1, pos2, out):
                 codes = ring.tile([P, S_GROUP], U32, name="x_codes", bufs=5, align_bytes=64)
                 scales = ring.tile([P, S_GROUP], U8, name="x_scales", bufs=5, align_bytes=64)
                 x_mx[grp, g] = (codes, scales)
-            quantise(x_bf[grp, g][:], x_mx[grp, g][0], x_mx[grp, g][1], s0, s1)
+            codes, scales = x_mx[grp, g]
+            nc.vector.quantize_mx(
+                out=codes[:, s0:s1].bitcast(FP8X4), scales=scales[:, s0:s1], in_=x_bf[grp, g, s0, s1]
+            )
 
         def multiply(grp, g, i, h):
             e = grp * E_GROUP + i
@@ -149,21 +150,21 @@ def tile_moe_pre_lin_gelu_kernel(tc, xT, w, b, gate, offs, pos1, pos2, out):
         load_gate(0, C)
         load_gate(C, S_GROUP)
         blocks = [(g, j) for g in range(PASSES) for j in range(PACK)]
-        matrices = [(0, g, i) for g in range(PASSES) for i in range(E_GROUP)]
-        lead = len(blocks) - len(matrices)
+        matrices = [(grp, g, i) for grp, g in steps for i in range(E_GROUP)]
+        loaded = 0
         for m, block in enumerate(blocks):
             if m > 0:
                 load_tokens(*block)
-            if m >= lead:
-                load_w(*matrices[m - lead])
+            if m not in (0, 3):
+                load_w(*matrices[loaded])
+                loaded += 1
         load_gate(S_GROUP, S)
         for h in range(HALVES):
             nc.sync.dma_start(bias_sb[h][:], b[h * P : (h + 1) * P, :])
         nc.sync.dma_start(pos_sb[0][:], pos1)
         nc.sync.dma_start(pos_sb[1][:], pos2)
-        for g in range(PASSES):
-            for i in range(E_GROUP):
-                load_w(1, g, i)
+        for matrix in matrices[loaded:]:
+            load_w(*matrix)
 
         def finish(grp, g):
             for s0, s1 in cuts_whole if (grp, g) == last else cuts_x:
@@ -174,11 +175,14 @@ def tile_moe_pre_lin_gelu_kernel(tc, xT, w, b, gate, offs, pos1, pos2, out):
                     multiply(grp, g, i, h)
 
         for n, (grp, g) in enumerate(steps):
-            gathered = ring.tile([P, PACK, S_GROUP], F32, name="planes")
-            for s0, s1 in [(0, C), (C, three), (0, two), (0, three)]:
+            gathered = ring.tile([P, PACK, S_GROUP], F32, name="planes", bufs=2)
+            rounded = ring.tile([P, S_GROUP * PACK], BF16, name="x_bf", bufs=2, align_bytes=64)
+            for s0, s1 in [(0, C), (C, three), (0, two), (two, three), (0, three)]:
                 planes[grp, g, s0, s1] = gathered[:, :, s0:s1]
+                x_bf[grp, g, s0, s1] = rounded[:, PACK * s0 : PACK * s1]
             if n == 0:
-                round_w(grp, g)
+                round_w(*steps[0])
+                round_w(*steps[1])
                 small = gather_x(grp, g, 0, C)
                 rest = gather_x(grp, g, C, three)
                 whole = gather_x(grp, g, 0, three)
@@ -191,12 +195,13 @@ def tile_moe_pre_lin_gelu_kernel(tc, xT, w, b, gate, offs, pos1, pos2, out):
             if (grp, g) != last:
                 for s0, s1 in cuts_x:
                     round_x(grp, g, s0, s1)
-                round_w(*steps[n + 1])
+            if n + 2 < len(steps):
+                round_w(*steps[n + 2])
             if n > 0:
                 finish(*steps[n - 1])
         grp, g = last
-        tail_planes = held.tile([P, PACK, C], F32, name="tail", align_bytes=64)
-        planes[grp, g, two, three] = tail_planes[:]
+        tail_bf = held.tile([P, C * PACK], BF16, name="tail", align_bytes=64)
+        x_bf[grp, g, two, three] = tail_bf[:]
         run_gathers(gather_x(grp, g, two, three))
         round_x(grp, g, two, three)
         finish(grp, g)
@@ -212,7 +217,7 @@ def tile_moe_pre_lin_gelu_kernel(tc, xT, w, b, gate, offs, pos1, pos2, out):
                 multiply(grp, g, i, 1)
 
         def fetch(h, t0, t1):
-            pair = ring.tile([P, 2, t1 - t0], F32, name="planes")
+            pair = ring.tile([P, 2, t1 - t0], F32, name="pair")
             for r in range(2):
                 nc.vector.tensor_copy(pair[:, r, :], y[h][:].indirect(pos_sb[r][:, t0 // STRIPE : t1 // STRIPE]))
             return pair

@@ -24,212 +24,178 @@ K_PASS = P * PACK
 PASSES = K // K_PASS
 HALVES = N // P
 STRIPE = 16
-GROUPS = 2
-E_GROUP = E // GROUPS
-S_GROUP = E_GROUP * C
-WINDOW = T + STRIPE
+WINDOW = S + STRIPE
 RUN = 4
+WORDS = P
+EARLY = [(e, 0) for e in range(E)] + [(0, 1), (1, 1)]
+LATE = [(e, 1) for e in range(2, E)]
+HEAD_SLOTS = 2 * C
+TAIL_FROM = 4 * C
 
 
 def tile_moe_pre_lin_gelu_kernel(tc, xT, w, b, gate, offs, pos1, pos2, out):
     nc = tc.nc
     with ExitStack() as ctx:
         held = ctx.enter_context(tc.tile_pool(name="held", bufs=1))
-        ring = ctx.enter_context(tc.tile_pool(name="ring", bufs=3))
+        ring = ctx.enter_context(tc.tile_pool(name="ring", bufs=2))
         psum = ctx.enter_context(tc.psum_pool(name="psum", bufs=8))
 
         offs_sb = held.tile([P, S // STRIPE], U16, name="offs_sb")
         pos_sb = [held.tile([P, T // STRIPE], U16, name="pos_sb%d" % r) for r in range(2)]
         gate_sb = held.tile([P, S], F32, name="gate_sb")
         bias_sb = [held.tile([P, E], F32, name="bias_sb%d" % h) for h in range(HALVES)]
-        tokens = [[held.tile([P, WINDOW], F32, name="tokens%d_%d" % (g, j)) for j in range(PACK)] for g in range(PASSES)]
         y = [held.tile([P, S], F32, name="y%d" % h) for h in range(HALVES)]
+        x_codes = held.tile([P, PASSES, S], U32, name="x_codes", align_bytes=64)
+        x_scales = held.tile([P, PASSES, S], U8, name="x_scales", align_bytes=64)
+        late_bf = held.tile([P, len(LATE), PASSES, P * PACK], BF16, name="late_bf", align_bytes=64)
+        late_scales = held.tile([P, len(LATE), PASSES * P], U8, name="late_scales", align_bytes=64)
 
-        w_late = held.tile([P, HALVES, PASSES, E_GROUP, P * PACK], BF16, name="w_late", align_bytes=64)
+        warm = held.tile([P, 2, 8], F32, name="warm")
+        nc.gpsimd.memset(warm[:, 0, :], 0.0)
+        nc.scalar.activation(warm[:, 1, :], warm[:, 0, :], GELU)
+
+        tokens = {}
         w_raw = {}
-        w_bf = {}
+        early_bf = {}
         w_mx = {}
-        planes = {}
-        x_bf = {}
-        x_mx = {}
         acc = {}
 
         def load_tokens(g, j):
+            tokens[g, j] = ring.tile([P, WINDOW], F32, name="tokens", bufs=5)
             rows = xT[g * K_PASS : (g + 1) * K_PASS, :].rearrange("(p j) t -> p j t", j=PACK)
-            nc.sync.dma_start(tokens[g][j][:, 0:T], rows[:, j, :])
+            nc.sync.dma_start(tokens[g, j][:, 0:T], rows[:, j, :])
 
         def load_gate(s0, s1):
             nc.sync.dma_start(gate_sb[:, s0:s1], gate[0:P, s0:s1])
 
-        def load_w(grp, g, i):
-            raw = ring.tile([P, PACK, N], F32, name="w_raw", bufs=9)
-            rows = w[grp * E_GROUP + i, g * K_PASS : (g + 1) * K_PASS, :]
-            nc.sync.dma_start(raw[:], rows.rearrange("(p j) n -> p j n", j=PACK))
-            w_raw[grp, g, i] = raw
+        def load_w(g, e):
+            w_raw[g, e] = ring.tile([P, PACK, N], F32, name="w_raw", bufs=7)
+            rows = w[e, g * K_PASS : (g + 1) * K_PASS, :]
+            nc.sync.dma_start(w_raw[g, e][:], rows.rearrange("(p j) n -> p j n", j=PACK))
 
-        def round_w(grp, g):
-            if grp == 0:
-                grouped = ring.tile([P, HALVES, E_GROUP, P * PACK], BF16, name="w_bf", bufs=3, align_bytes=64)
-                w_bf[grp, g] = grouped[:].rearrange("p h i c -> p (h i c)")
-            else:
-                grouped = w_late[:, :, g, :, :]
-                w_bf[grp, g] = w_late[:, 0, g, :, :].rearrange("p i c -> p (i c)")
-            for i in range(E_GROUP):
-                nc.scalar.copy(
-                    grouped[:, :, i, :].rearrange("p h (c r j) -> p h c j r", r=RUN, j=PACK),
-                    w_raw[grp, g, i][:].rearrange("p j (h c r) -> p h c j r", h=HALVES, r=RUN),
-                )
-
-        def quantise(values, codes, scales, c0, c1):
-            nc.vector.quantize_mx(
-                out=codes[:, c0:c1].bitcast(FP8X4), scales=scales[:, c0:c1], in_=values[:, PACK * c0 : PACK * c1]
-            )
-
-        def quantise_w(grp, g, cuts):
-            codes = ring.tile([P, E_GROUP * N], U32, name="w_codes", align_bytes=64)
-            scales = ring.tile([P, E_GROUP * N], U8, name="w_scales", align_bytes=64)
-            for h in range(HALVES):
-                cols = slice(h * E_GROUP * P, (h + 1) * E_GROUP * P)
-                w_mx[grp, g, h] = (codes[:, cols], scales[:, cols])
-            for c0, c1 in cuts:
-                quantise(w_bf[grp, g], codes, scales, c0, c1)
-
-        def gather_x(grp, g, s0, s1):
-            a0, a1 = grp * S_GROUP + s0, grp * S_GROUP + s1
-            return [(planes[grp, g, s0, s1][:, j, :], tokens[g][j], a0, a1) for j in range(PACK)]
-
-        def run_gathers(jobs):
-            for dst, window, a0, a1 in jobs:
-                picked = window[:].indirect(offs_sb[:, a0 // STRIPE : a1 // STRIPE])
-                nc.vector.tensor_tensor(dst, picked, gate_sb[:, a0:a1], MULT)
-
-        def round_x(grp, g, s0, s1):
+        def round_and_interleave(dst, src):
             nc.scalar.copy(
-                x_bf[grp, g, s0, s1].rearrange("p (c r j) -> p c j r", r=RUN, j=PACK),
-                planes[grp, g, s0, s1].rearrange("p j (c r) -> p c j r", r=RUN),
+                dst.rearrange("p (c r j) -> p c j r", r=RUN, j=PACK), src.rearrange("p j (c r) -> p c j r", r=RUN)
             )
 
-        def quantise_x(grp, g, s0, s1):
-            if (grp, g) not in x_mx:
-                codes = ring.tile([P, S_GROUP], U32, name="x_codes", bufs=5, align_bytes=64)
-                scales = ring.tile([P, S_GROUP], U8, name="x_scales", bufs=5, align_bytes=64)
-                x_mx[grp, g] = (codes, scales)
-            codes, scales = x_mx[grp, g]
-            nc.vector.quantize_mx(
-                out=codes[:, s0:s1].bitcast(FP8X4), scales=scales[:, s0:s1], in_=x_bf[grp, g, s0, s1]
-            )
+        def quantise(codes, scales, values):
+            nc.vector.quantize_mx(out=codes.bitcast(FP8X4), scales=scales, in_=values)
 
-        def multiply(grp, g, i, h):
-            e = grp * E_GROUP + i
+        def round_w(g):
+            early_bf[g] = ring.tile([P, len(EARLY), P * PACK], BF16, name="early_bf", align_bytes=64)
+            for e in range(E):
+                for h in range(HALVES):
+                    if (e, h) in EARLY:
+                        dst = early_bf[g][:, EARLY.index((e, h)), :]
+                    else:
+                        dst = late_bf[:, LATE.index((e, h)), g, :]
+                    round_and_interleave(dst, w_raw[g, e][:, :, h * P : (h + 1) * P])
+
+        def quantise_early_w(g):
+            codes = ring.tile([P, len(EARLY) * P], U32, name="early_codes", align_bytes=64)
+            scales = ring.tile([P, len(EARLY) * P], U8, name="early_scales", align_bytes=64)
+            quantise(codes[:], scales[:], early_bf[g][:].rearrange("p m c -> p (m c)"))
+            for m, (e, h) in enumerate(EARLY):
+                w_mx[g, e, h] = (codes[:, m * P : (m + 1) * P], scales[:, m * P : (m + 1) * P])
+
+        def gather(planes, g, j, s0, s1):
+            picked = tokens[g, j][:].indirect(offs_sb[:, s0 // STRIPE : s1 // STRIPE])
+            nc.vector.tensor_tensor(planes[:, j, s0:s1], picked, gate_sb[:, s0:s1], MULT)
+
+        def multiply(g, e, h):
             if g == 0:
                 acc[e, h] = psum.tile([P, C], F32, name="acc")
-            w_cols = slice(i * P, (i + 1) * P)
-            x_cols = slice(i * C, (i + 1) * C)
+            slots = slice(e * C, (e + 1) * C)
             nc.tensor.matmul_mx(
                 out=acc[e, h][:],
-                lhsT=w_mx[grp, g, h][0][:, w_cols].bitcast(FP8X4),
-                lhsT_scale=w_mx[grp, g, h][1][:, w_cols],
-                rhs=x_mx[grp, g][0][:, x_cols].bitcast(FP8X4),
-                rhs_scale=x_mx[grp, g][1][:, x_cols],
+                lhsT=w_mx[g, e, h][0].bitcast(FP8X4),
+                lhsT_scale=w_mx[g, e, h][1],
+                rhs=x_codes[:, g, slots].bitcast(FP8X4),
+                rhs_scale=x_scales[:, g, slots],
                 start=(g == 0),
                 stop=(g == PASSES - 1),
             )
             if g == PASSES - 1:
-                nc.scalar.activation(y[h][:, e * C : (e + 1) * C], acc[e, h][:], GELU, bias=bias_sb[h][:, e : e + 1])
+                nc.scalar.activation(y[h][:, slots], acc[e, h][:], GELU, bias=bias_sb[h][:, e : e + 1])
 
-        two, three = 2 * C, 3 * C
-        half = E_GROUP * P
-        cuts_whole = [(0, two), (two, three)]
-        cuts_x = [(0, C), (C, three)]
-        cuts_first = [(0, C), (C, half)]
-        last = (GROUPS - 1, PASSES - 1)
-        steps = [(grp, g) for grp in range(GROUPS) for g in range(PASSES)]
-
+        blocks = [(g, j) for g in range(PASSES) for j in range(PACK)]
+        matrices = [(g, e) for g in range(PASSES) for e in range(E)]
         load_tokens(0, 0)
         nc.sync.dma_start(offs_sb[:], offs)
-        load_gate(0, C)
-        load_gate(C, S_GROUP)
-        blocks = [(g, j) for g in range(PASSES) for j in range(PACK)]
-        matrices = [(grp, g, i) for grp, g in steps for i in range(E_GROUP)]
+        load_gate(0, HEAD_SLOTS)
+        load_gate(HEAD_SLOTS, S)
+        ahead = [1, 2, 2, 0, 0, 4, 4, 0, 0, 4, 4, 0, 0, 3, 0]
         loaded = 0
-        for m, block in enumerate(blocks):
-            if m > 0:
-                load_tokens(*block)
-            if m not in (0, 3):
-                load_w(*matrices[loaded])
-                loaded += 1
-        load_gate(S_GROUP, S)
+        for block, count in zip(blocks[1:], ahead):
+            for matrix in matrices[loaded : loaded + count]:
+                load_w(*matrix)
+            loaded += count
+            load_tokens(*block)
         for h in range(HALVES):
             nc.sync.dma_start(bias_sb[h][:], b[h * P : (h + 1) * P, :])
         nc.sync.dma_start(pos_sb[0][:], pos1)
         nc.sync.dma_start(pos_sb[1][:], pos2)
-        for matrix in matrices[loaded:]:
-            load_w(*matrix)
 
-        def finish(grp, g):
-            for s0, s1 in cuts_whole if (grp, g) == last else cuts_x:
-                quantise_x(grp, g, s0, s1)
-            quantise_w(grp, g, cuts_whole if grp == 0 else cuts_first)
-            for i in range(E_GROUP):
-                for h in range(HALVES if grp == 0 else 1):
-                    multiply(grp, g, i, h)
+        cuts = [(0, TAIL_FROM), (TAIL_FROM, S)]
+        x_bf = {}
 
-        for n, (grp, g) in enumerate(steps):
-            gathered = ring.tile([P, PACK, S_GROUP], F32, name="planes", bufs=2)
-            rounded = ring.tile([P, S_GROUP * PACK], BF16, name="x_bf", bufs=2, align_bytes=64)
-            for s0, s1 in [(0, C), (C, three), (0, two), (two, three), (0, three)]:
-                planes[grp, g, s0, s1] = gathered[:, :, s0:s1]
-                x_bf[grp, g, s0, s1] = rounded[:, PACK * s0 : PACK * s1]
-            if n == 0:
-                round_w(*steps[0])
-                round_w(*steps[1])
-                small = gather_x(grp, g, 0, C)
-                rest = gather_x(grp, g, C, three)
-                whole = gather_x(grp, g, 0, three)
-                run_gathers([small[0], rest[0]] + whole[1:])
-            elif (grp, g) == last:
-                run_gathers(gather_x(grp, g, 0, two))
-                round_x(grp, g, 0, two)
-            else:
-                run_gathers(gather_x(grp, g, 0, three))
-            if (grp, g) != last:
-                for s0, s1 in cuts_x:
-                    round_x(grp, g, s0, s1)
-            if n + 2 < len(steps):
-                round_w(*steps[n + 2])
-            if n > 0:
-                finish(*steps[n - 1])
-        grp, g = last
-        tail_bf = held.tile([P, C * PACK], BF16, name="tail", align_bytes=64)
-        x_bf[grp, g, two, three] = tail_bf[:]
-        run_gathers(gather_x(grp, g, two, three))
-        round_x(grp, g, two, three)
-        finish(grp, g)
-        late_codes = held.tile([P, PASSES * half], U32, name="tail", align_bytes=64)
-        late_scales = held.tile([P, PASSES * half], U8, name="late_scales", align_bytes=64)
-        late_values = w_late[:, 1, :, :, :].rearrange("p g i c -> p (g i c)")
-        for c0 in range(0, PASSES * half, C):
-            quantise(late_values, late_codes, late_scales, c0, c0 + C)
+        def finish(g):
+            for s0, s1 in cuts:
+                quantise(x_codes[:, g, s0:s1], x_scales[:, g, s0:s1], x_bf[g, s0])
+            quantise_early_w(g)
+            for e, h in EARLY:
+                multiply(g, e, h)
+
+        round_w(0)
+        round_w(1)
         for g in range(PASSES):
-            cols = slice(g * half, (g + 1) * half)
-            w_mx[grp, g, 1] = (late_codes[:, cols], late_scales[:, cols])
-            for i in range(E_GROUP):
-                multiply(grp, g, i, 1)
+            planes = ring.tile([P, PACK, S], F32, name="planes")
+            rounded = ring.tile([P, S * PACK], BF16, name="x_bf", align_bytes=64)
+            for s0, s1 in cuts:
+                x_bf[g, s0] = rounded[:, PACK * s0 : PACK * s1]
+            if g < PASSES - 1:
+                for j in range(PACK):
+                    if (g, j) == (0, 0):
+                        gather(planes, g, j, 0, HEAD_SLOTS)
+                        gather(planes, g, j, HEAD_SLOTS, S)
+                    else:
+                        gather(planes, g, j, 0, S)
+            else:
+                tail_bf = held.tile([P, (S - TAIL_FROM) * PACK], BF16, name="tail", align_bytes=64)
+                x_bf[g, TAIL_FROM] = tail_bf[:]
+                for s0, s1 in cuts:
+                    for j in range(PACK):
+                        gather(planes, g, j, s0, s1)
+            for s0, s1 in cuts:
+                round_and_interleave(x_bf[g, s0], planes[:, :, s0:s1])
+            if g + 2 < PASSES:
+                round_w(g + 2)
+            if g > 0:
+                finish(g - 1)
+        finish(PASSES - 1)
 
-        def fetch(h, t0, t1):
-            pair = ring.tile([P, 2, t1 - t0], F32, name="pair")
-            for r in range(2):
-                nc.vector.tensor_copy(pair[:, r, :], y[h][:].indirect(pos_sb[r][:, t0 // STRIPE : t1 // STRIPE]))
-            return pair
+        late_codes = held.tile([P, len(LATE), PASSES * P], U32, name="tail", align_bytes=64)
+        for m, (e, h) in enumerate(LATE):
+            quantise(late_codes[:, m, :], late_scales[:, m, :], late_bf[:, m, :, :].rearrange("p g c -> p (g c)"))
+            for g in range(PASSES):
+                w_mx[g, e, h] = (late_codes[:, m, g * P : (g + 1) * P], late_scales[:, m, g * P : (g + 1) * P])
+                multiply(g, e, h)
+
+        def fetch(pair, r, h, t0, t1):
+            nc.vector.tensor_copy(pair[:, r, :], y[h][:].indirect(pos_sb[r][:, t0 // STRIPE : t1 // STRIPE]))
 
         def add_and_store(pair, h, t0, t1):
-            nc.vector.tensor_tensor(pair[:, 0, :], pair[:, 0, :], pair[:, 1, :], ADD)
-            nc.sync.dma_start(out[h * P : (h + 1) * P, t0:t1], pair[:, 0, :])
+            total = ring.tile([P, t1 - t0], F32, name="w_raw", bufs=7)
+            nc.vector.tensor_tensor(total[:], pair[:, 0, :], pair[:, 1, :], ADD)
+            nc.sync.dma_start(out[h * P : (h + 1) * P, t0:t1], total[:])
 
-        pieces = [(0, 0, T), (1, 0, two), (1, two, T)]
+        pieces = [(0, 0, T), (1, 0, 2 * C), (1, 2 * C, T)]
         pairs = []
-        for n, piece in enumerate(pieces):
-            pairs.append(fetch(*piece))
+        for n, (h, t0, t1) in enumerate(pieces):
+            pair = ring.tile([P, 2, t1 - t0], F32, name="x_bf", align_bytes=64)
+            pairs.append(pair)
+            fetch(pair, 0, h, t0, t1)
             if n > 0:
                 add_and_store(pairs[n - 1], *pieces[n - 1])
+            fetch(pair, 1, h, t0, t1)
         add_and_store(pairs[-1], *pieces[-1])

from contextlib import ExitStack

import concourse.mybir as mybir

K, T, E, C, N = 2048, 768, 6, 256, 256
S = E * C

FLOPS = 2 * K * N * S
BYTES = 4 * (K * T + E * K * N + N * E + S + N * T) + 2 * (S + 2 * T)

F32 = mybir.dt.float32
BF16 = mybir.dt.bfloat16
U32 = mybir.dt.uint32
U16 = mybir.dt.uint16
U8 = mybir.dt.uint8
FP8X4 = mybir.dt.float8_e4m3fn_x4
MULT = mybir.AluOpType.mult
ADD = mybir.AluOpType.add
GELU = mybir.ActivationFunctionType.Gelu_apprx_tanh

P = 128
PACK = 4
K_PASS = P * PACK
PASSES = K // K_PASS
HALVES = N // P
STRIPE = 16
WINDOW = S + STRIPE
RUN = 4
WORDS = P
EARLY = [(e, 0) for e in range(E)] + [(0, 1), (1, 1)]
LATE = [(e, 1) for e in range(2, E)]
HEAD_SLOTS = 2 * C
TAIL_FROM = 4 * C


def tile_moe_pre_lin_gelu_kernel(tc, xT, w, b, gate, offs, pos1, pos2, out):
    nc = tc.nc
    with ExitStack() as ctx:
        held = ctx.enter_context(tc.tile_pool(name="held", bufs=1))
        ring = ctx.enter_context(tc.tile_pool(name="ring", bufs=2))
        psum = ctx.enter_context(tc.psum_pool(name="psum", bufs=8))

        offs_sb = held.tile([P, S // STRIPE], U16, name="offs_sb")
        pos_sb = [held.tile([P, T // STRIPE], U16, name="pos_sb%d" % r) for r in range(2)]
        gate_sb = held.tile([P, S], F32, name="gate_sb")
        bias_sb = [held.tile([P, E], F32, name="bias_sb%d" % h) for h in range(HALVES)]
        y = [held.tile([P, S], F32, name="y%d" % h) for h in range(HALVES)]
        x_codes = held.tile([P, PASSES, S], U32, name="x_codes", align_bytes=64)
        x_scales = held.tile([P, PASSES, S], U8, name="x_scales", align_bytes=64)
        late_bf = held.tile([P, len(LATE), PASSES, P * PACK], BF16, name="late_bf", align_bytes=64)
        late_scales = held.tile([P, len(LATE), PASSES * P], U8, name="late_scales", align_bytes=64)

        warm = held.tile([P, 2, 8], F32, name="warm")
        nc.gpsimd.memset(warm[:, 0, :], 0.0)
        nc.scalar.activation(warm[:, 1, :], warm[:, 0, :], GELU)

        tokens = {}
        w_raw = {}
        early_bf = {}
        w_mx = {}
        acc = {}

        def load_tokens(g, j):
            tokens[g, j] = ring.tile([P, WINDOW], F32, name="tokens", bufs=5)
            rows = xT[g * K_PASS : (g + 1) * K_PASS, :].rearrange("(p j) t -> p j t", j=PACK)
            nc.sync.dma_start(tokens[g, j][:, 0:T], rows[:, j, :])

        def load_gate(s0, s1):
            nc.sync.dma_start(gate_sb[:, s0:s1], gate[0:P, s0:s1])

        def load_w(g, e):
            w_raw[g, e] = ring.tile([P, PACK, N], F32, name="w_raw", bufs=7)
            rows = w[e, g * K_PASS : (g + 1) * K_PASS, :]
            nc.sync.dma_start(w_raw[g, e][:], rows.rearrange("(p j) n -> p j n", j=PACK))

        def round_and_interleave(dst, src):
            nc.scalar.copy(
                dst.rearrange("p (c r j) -> p c j r", r=RUN, j=PACK), src.rearrange("p j (c r) -> p c j r", r=RUN)
            )

        def quantise(codes, scales, values):
            nc.vector.quantize_mx(out=codes.bitcast(FP8X4), scales=scales, in_=values)

        def round_w(g):
            early_bf[g] = ring.tile([P, len(EARLY), P * PACK], BF16, name="early_bf", align_bytes=64)
            for e in range(E):
                for h in range(HALVES):
                    if (e, h) in EARLY:
                        dst = early_bf[g][:, EARLY.index((e, h)), :]
                    else:
                        dst = late_bf[:, LATE.index((e, h)), g, :]
                    round_and_interleave(dst, w_raw[g, e][:, :, h * P : (h + 1) * P])

        def quantise_early_w(g):
            codes = ring.tile([P, len(EARLY) * P], U32, name="early_codes", align_bytes=64)
            scales = ring.tile([P, len(EARLY) * P], U8, name="early_scales", align_bytes=64)
            quantise(codes[:], scales[:], early_bf[g][:].rearrange("p m c -> p (m c)"))
            for m, (e, h) in enumerate(EARLY):
                w_mx[g, e, h] = (codes[:, m * P : (m + 1) * P], scales[:, m * P : (m + 1) * P])

        def gather(planes, g, j, s0, s1):
            picked = tokens[g, j][:].indirect(offs_sb[:, s0 // STRIPE : s1 // STRIPE])
            nc.vector.tensor_tensor(planes[:, j, s0:s1], picked, gate_sb[:, s0:s1], MULT)

        def multiply(g, e, h):
            if g == 0:
                acc[e, h] = psum.tile([P, C], F32, name="acc")
            slots = slice(e * C, (e + 1) * C)
            nc.tensor.matmul_mx(
                out=acc[e, h][:],
                lhsT=w_mx[g, e, h][0].bitcast(FP8X4),
                lhsT_scale=w_mx[g, e, h][1],
                rhs=x_codes[:, g, slots].bitcast(FP8X4),
                rhs_scale=x_scales[:, g, slots],
                start=(g == 0),
                stop=(g == PASSES - 1),
            )
            if g == PASSES - 1:
                nc.scalar.activation(y[h][:, slots], acc[e, h][:], GELU, bias=bias_sb[h][:, e : e + 1])

        blocks = [(g, j) for g in range(PASSES) for j in range(PACK)]
        matrices = [(g, e) for g in range(PASSES) for e in range(E)]
        load_tokens(0, 0)
        nc.sync.dma_start(offs_sb[:], offs)
        load_gate(0, HEAD_SLOTS)
        load_gate(HEAD_SLOTS, S)
        ahead = [1, 2, 2, 0, 0, 4, 4, 0, 0, 4, 4, 0, 0, 3, 0]
        loaded = 0
        for block, count in zip(blocks[1:], ahead):
            for matrix in matrices[loaded : loaded + count]:
                load_w(*matrix)
            loaded += count
            load_tokens(*block)
        for h in range(HALVES):
            nc.sync.dma_start(bias_sb[h][:], b[h * P : (h + 1) * P, :])
        nc.sync.dma_start(pos_sb[0][:], pos1)
        nc.sync.dma_start(pos_sb[1][:], pos2)

        cuts = [(0, TAIL_FROM), (TAIL_FROM, S)]
        x_bf = {}

        def finish(g):
            for s0, s1 in cuts:
                quantise(x_codes[:, g, s0:s1], x_scales[:, g, s0:s1], x_bf[g, s0])
            quantise_early_w(g)
            for e, h in EARLY:
                multiply(g, e, h)

        round_w(0)
        round_w(1)
        for g in range(PASSES):
            planes = ring.tile([P, PACK, S], F32, name="planes")
            rounded = ring.tile([P, S * PACK], BF16, name="x_bf", align_bytes=64)
            for s0, s1 in cuts:
                x_bf[g, s0] = rounded[:, PACK * s0 : PACK * s1]
            if g < PASSES - 1:
                for j in range(PACK):
                    if (g, j) == (0, 0):
                        gather(planes, g, j, 0, HEAD_SLOTS)
                        gather(planes, g, j, HEAD_SLOTS, S)
                    else:
                        gather(planes, g, j, 0, S)
            else:
                tail_bf = held.tile([P, (S - TAIL_FROM) * PACK], BF16, name="tail", align_bytes=64)
                x_bf[g, TAIL_FROM] = tail_bf[:]
                for s0, s1 in cuts:
                    for j in range(PACK):
                        gather(planes, g, j, s0, s1)
            for s0, s1 in cuts:
                round_and_interleave(x_bf[g, s0], planes[:, :, s0:s1])
            if g + 2 < PASSES:
                round_w(g + 2)
            if g > 0:
                finish(g - 1)
        finish(PASSES - 1)

        late_codes = held.tile([P, len(LATE), PASSES * P], U32, name="tail", align_bytes=64)
        for m, (e, h) in enumerate(LATE):
            quantise(late_codes[:, m, :], late_scales[:, m, :], late_bf[:, m, :, :].rearrange("p g c -> p (g c)"))
            for g in range(PASSES):
                w_mx[g, e, h] = (late_codes[:, m, g * P : (g + 1) * P], late_scales[:, m, g * P : (g + 1) * P])
                multiply(g, e, h)

        def fetch(pair, r, h, t0, t1):
            nc.vector.tensor_copy(pair[:, r, :], y[h][:].indirect(pos_sb[r][:, t0 // STRIPE : t1 // STRIPE]))

        def add_and_store(pair, h, t0, t1):
            total = ring.tile([P, t1 - t0], F32, name="w_raw", bufs=7)
            nc.vector.tensor_tensor(total[:], pair[:, 0, :], pair[:, 1, :], ADD)
            nc.sync.dma_start(out[h * P : (h + 1) * P, t0:t1], total[:])

        pieces = [(0, 0, T), (1, 0, 2 * C), (1, 2 * C, T)]
        pairs = []
        for n, (h, t0, t1) in enumerate(pieces):
            pair = ring.tile([P, 2, t1 - t0], F32, name="x_bf", align_bytes=64)
            pairs.append(pair)
            fetch(pair, 0, h, t0, t1)
            if n > 0:
                add_and_store(pairs[n - 1], *pieces[n - 1])
            fetch(pair, 1, h, t0, t1)
        add_and_store(pairs[-1], *pieces[-1])
